import numpy as np
import ml_dtypes


def mxq(x, axis, fmt="e4m3"):
    dtype, down = {"e4m3": (ml_dtypes.float8_e4m3fn, 7), "e5m2": (ml_dtypes.float8_e5m2, 14)}[fmt]
    v = np.moveaxis(np.asarray(x, np.float32).astype(ml_dtypes.bfloat16).astype(np.float64), axis, -1)
    blocks = v.reshape(v.shape[:-1] + (-1, 32))
    amax = np.abs(blocks).max(-1, keepdims=True)
    byte = np.maximum(np.where(amax > 0, np.frexp(amax)[1] - 1 + 127, 0) - down, 1)
    scale = np.exp2(byte - 127.0)
    codes = (blocks / scale).astype(np.float32).astype(dtype).astype(np.float64)
    return np.moveaxis((codes * scale).reshape(v.shape), -1, axis)


WIDE = False


def mx_kscale(k, group=512):
    if not WIDE:
        return np.ones(k)
    levels = np.array([10, -10, 5, -5, 0])
    if group != 512:
        return np.exp2(np.random.permutation(np.resize(levels, k // group))).repeat(group)
    if k % 512:
        return np.exp2(np.random.permutation(np.resize(levels, k // 32))).repeat(32)
    a = np.empty((k // 512, 16))
    for p in range(k // 512):
        a[p, :8] = np.random.permutation(np.resize(levels, 8))
        for g in range(8):
            far = levels[np.abs(levels - a[p, g]) >= 10]
            a[p, g + 8] = far[np.random.randint(len(far))]
    return np.exp2(a.ravel()).repeat(32)


def f64(x):
    return np.asarray(x).astype(np.float64)


G, D, M, O, N = 2, 256, 128, 256, 512


def setup_inputs():
    n = np.random.standard_normal
    s_d = mx_kscale(D, 0)
    s_o = mx_kscale(O, 0)
    return {
        "x": (n((G, D, N)) * s_d[:, None]).astype(np.float32),
        "w1": (n((G, D, M)) / np.sqrt(D) / s_d[:, None]).astype(np.float32),
        "w2": (n((G, D, M)) / np.sqrt(D) / s_d[:, None]).astype(np.float32),
        "w3": (n((G, D, M)) / np.sqrt(D) / s_d[:, None]).astype(np.float32),
        "re": (np.random.uniform(0.3, 1.5, (G, M, 1))).astype(np.float32),
        "wo": (n((G, O, M)) / np.sqrt(O) / s_o[:, None]).astype(np.float32),
        "dy": (n((G, O, N)) * s_o[:, None]).astype(np.float32),
        "og": (np.random.uniform(0.3, 1.0, (G, M, 1))).astype(np.float32),
        "base": (0.2 * n((G, M, N))).astype(np.float32),
    }


def reference(x, w1, w2, w3, re, wo, dy, og, base):
    w1q = mxq(f64(w1), 1, "e4m3")
    xq = mxq(f64(x), 1, "e4m3")
    z1 = w1q.transpose(0, 2, 1) @ xq
    w2q = mxq(f64(w2), 1, "e4m3")
    z2 = w2q.transpose(0, 2, 1) @ xq
    w3q = mxq(f64(w3), 1, "e4m3")
    z3 = w3q.transpose(0, 2, 1) @ xq
    e1 = np.exp(z1)
    e2 = np.exp(z2)
    woq = mxq(f64(wo), 1, "e4m3")
    dyq = mxq(f64(dy), 1, "e4m3")
    c0 = woq.transpose(0, 2, 1) @ dyq
    de1 = c0 * z3 / (e1 + e2 + f64(re)) - c0 * z3 * e1 / np.square(e1 + e2 + f64(re))
    dz1 = de1 * e1
    kdz1 = dz1 * 2.0
    kde1 = kdz1 * e1
    ke1 = kdz1 * de1 + kde1 * (-1.0) / np.square(e1 + e2 + f64(re)) * c0 * z3 + kde1 * (-1.0) * c0 * z3 * e1 / np.square(np.square(e1 + e2 + f64(re))) * (-1.0) * (e1 + e2 + f64(re)) * 2.0 - kde1 * c0 * z3 / np.square(e1 + e2 + f64(re))
    kz1 = ke1 * e1
    y = kz1 * f64(og) + f64(base)
    return y

@@ -1,0 +1,201 @@
+from contextlib import ExitStack
+
+import concourse.mybir as mybir
+
+F32 = mybir.dt.float32
+BF16 = mybir.dt.bfloat16
+U32 = mybir.dt.uint32
+U8 = mybir.dt.uint8
+FP8X4 = mybir.dt.float8_e4m3fn_x4
+ACT = mybir.ActivationFunctionType
+ALU = mybir.AluOpType
+
+G, D, M, N = 2, 256, 128, 512
+P = 128
+PACK = 4
+ROWS = D // PACK
+HALF = N // 2
+NT = 128
+SCALAR_COLS = 80
+
+FLOPS = 4 * 2 * G * D * M * N
+
+
+def tile_rows_gptwoshare_kernel(tc, x, w1, w2, w3, re, wo, dy, og, base, out):
+    nc = tc.nc
+    with ExitStack() as ctx:
+        sb = ctx.enter_context(tc.tile_pool(name="sb", bufs=1))
+        ps = ctx.enter_context(tc.psum_pool(name="ps", bufs=1))
+        ctx.enter_context(tc.manual_schedule())
+
+        def load(name, src, c0, width):
+            raw = sb.tile([P, PACK, width], F32, name=name, align_bytes=64)
+            view = src.rearrange("g (p j) c -> (g p) j c", j=PACK)
+            nc.sync.dma_start(out=raw[:], in_=view[:, :, c0 : c0 + width])
+            return raw
+
+        def operand(name, width):
+            grouped = sb.tile([P, width, PACK], BF16, name=name + "_b", align_bytes=64)
+            codes = sb.tile([P, width], U32, name=name + "_c", align_bytes=64)
+            scales = sb.tile([P, width], U8, name=name + "_s", align_bytes=64)
+            return grouped, codes, scales
+
+        def views(op, raw, dst0, c0, c1):
+            dst = op[0][:, dst0 + c0 : dst0 + c1, :].rearrange("p (c i) j -> p c j i", i=4)
+            src = raw[:, :, c0:c1].rearrange("p j (c i) -> p c j i", i=4)
+            return dst, src
+
+        def inter_v(op, raw, dst0, c0, c1):
+            dst, src = views(op, raw, dst0, c0, c1)
+            nc.vector.tensor_copy(out=dst, in_=src)
+
+        def inter_s(op, raw, dst0, c0, c1):
+            dst, src = views(op, raw, dst0, c0, c1)
+            nc.scalar.copy(out=dst, in_=src)
+
+        def quantise(op):
+            nc.vector.quantize_mx(
+                out=op[1][:].bitcast(FP8X4), scales=op[2][:], in_=op[0][:].rearrange("p c j -> p (c j)")
+            )
+
+        def mm(dst, g, wop, w0, aop, a0, start, stop):
+            rows = slice(g * ROWS, (g + 1) * ROWS)
+            nc.tensor.matmul_mx(
+                out=dst,
+                lhsT=wop[1][rows, w0 : w0 + M].bitcast(FP8X4),
+                lhsT_scale=wop[2][rows, w0 : w0 + M],
+                rhs=aop[1][rows, a0 : a0 + NT].bitcast(FP8X4),
+                rhs_scale=aop[2][rows, a0 : a0 + NT],
+                start=start,
+                stop=stop,
+            )
+
+        re_t = sb.tile([P, G, 8], F32, name="re_t")
+        og_t = sb.tile([P, G, 8], F32, name="og_t")
+        with nc.allow_non_contiguous_dma(reason="one value a partition"):
+            nc.scalar.dma_start(out=re_t[:, :, 0:1], in_=re.rearrange("g m o -> m g o"))
+            nc.scalar.dma_start(out=og_t[:, :, 0:1], in_=og.rearrange("g m o -> m g o"))
+
+        w1_raw = load("w1_raw", w1, 0, M)
+        w2_raw = load("w2_raw", w2, 0, M)
+        x_raw = [load("x_raw%d" % h, x, h * HALF, HALF) for h in range(2)]
+        w3_raw = load("w3_raw", w3, 0, M)
+        wo_raw = load("wo_raw", wo, 0, M)
+        dy_raw = [load("dy_raw%d" % h, dy, h * HALF, HALF) for h in range(2)]
+        base_t = sb.tile([P, G, N], F32, name="base_t")
+        nc.sync.dma_start(out=base_t[:], in_=base.rearrange("g m n -> m g n"))
+
+        w12 = operand("w12", 2 * M)
+        w3o = operand("w3o", 2 * M)
+        xq = [operand("xq%d" % h, HALF) for h in range(2)]
+        dyq = [operand("dyq%d" % h, HALF) for h in range(2)]
+
+        chunks = [(h, g) for h in range(2) for g in range(G)]
+        e_bank = {c: ps.tile([P, 2 * HALF], F32, name="e_bank%d%d" % c) for c in chunks}
+        a_bank = {c: ps.tile([P, 2 * HALF], F32, name="a_bank%d%d" % c) for c in chunks}
+
+        def work(name, width=HALF):
+            return {c: sb.tile([P, width], F32, name=name + "%d%d" % c) for c in chunks}
+
+        e_t = work("e", 2 * HALF)
+        t_t, rs_t, p_t, h2_t = work("t"), work("rs"), work("p"), work("h2")
+        g1_t, g2_t, gg_t, hh_t, y_t = work("g1"), work("g2"), work("gg"), work("hh"), work("y")
+        gain = sb.tile([P, G, 8], F32, name="gain")
+
+        def score_matmuls(h):
+            for g in range(G):
+                bank = e_bank[(h, g)]
+                for b in range(HALF // NT):
+                    mm(bank[:, b * NT : (b + 1) * NT], g, w12, 0, xq[h], b * NT, True, True)
+                for b in range(HALF // NT):
+                    dst = bank[:, HALF + b * NT : HALF + (b + 1) * NT]
+                    mm(dst, g, w12, 0, xq[h], b * NT, True, False)
+                    mm(dst, g, w12, M, xq[h], b * NT, False, True)
+
+        def value_matmuls(h, which, aop):
+            for g in range(G):
+                for b in range(HALF // NT):
+                    dst = a_bank[(h, g)][:, which * HALF + b * NT : which * HALF + (b + 1) * NT]
+                    mm(dst, g, w3o, which * M, aop, b * NT, True, True)
+
+        def exps(h):
+            for g in range(G):
+                nc.scalar.activation(out=e_t[(h, g)][:], in_=e_bank[(h, g)][:], func=ACT.Exp)
+
+        def odds(h):
+            for g in range(G):
+                c = (h, g)
+                nc.vector.scalar_tensor_tensor(
+                    out=t_t[c][:], in0=e_t[c][:, 0:HALF], scalar=re_t[:, g, 0:1], in1=e_t[c][:, HALF : 2 * HALF],
+                    op0=ALU.mult, op1=ALU.add,
+                )
+
+        nc.vector.tensor_scalar(
+            out=w12[0][:, 0:M, :], in0=w1_raw[:].rearrange("p j c -> p c j"), scalar1=-1.0, scalar2=None, op0=ALU.mult
+        )
+        inter_s(w12, w2_raw, M, 0, M)
+        nc.gpsimd.tensor_scalar(out=gain[:, :, 0:1], in0=og_t[:, :, 0:1], scalar1=-4.0, scalar2=None, op0=ALU.mult)
+        quantise(w12)
+        for h in range(2):
+            inter_v(xq[h], x_raw[h], 0, SCALAR_COLS, HALF)
+            inter_s(xq[h], x_raw[h], 0, 0, SCALAR_COLS)
+            quantise(xq[h])
+            score_matmuls(h)
+        exps(0)
+        exps(1)
+        inter_v(w3o, w3_raw, 0, 0, M)
+        inter_v(w3o, wo_raw, M, 0, M)
+        odds(0)
+        quantise(w3o)
+        value_matmuls(0, 0, xq[0])
+        value_matmuls(1, 0, xq[1])
+        inter_v(dyq[0], dy_raw[0], 0, 0, HALF)
+        odds(1)
+        quantise(dyq[0])
+        value_matmuls(0, 1, dyq[0])
+        inter_v(dyq[1], dy_raw[1], 0, 0, HALF)
+        quantise(dyq[1])
+        value_matmuls(1, 1, dyq[1])
+
+        def root(c):
+            nc.scalar.activation(out=rs_t[c][:], in_=t_t[c][:], func=ACT.Abs_reciprocal_sqrt, bias=1.0)
+
+        def share(c):
+            nc.scalar.activation(out=p_t[c][:], in_=rs_t[c][:], func=ACT.Square)
+
+        def centred(c):
+            nc.scalar.activation(out=h2_t[c][:], in_=p_t[c][:], func=ACT.Square, bias=-0.5)
+
+        def first(c):
+            nc.vector.scalar_tensor_tensor(
+                out=g1_t[c][:], in0=h2_t[c][:], scalar=-0.25, in1=a_bank[c][:, 0:HALF], op0=ALU.add, op1=ALU.mult
+            )
+
+        def second(c):
+            nc.vector.tensor_tensor(out=g2_t[c][:], in0=g1_t[c][:], in1=a_bank[c][:, HALF : 2 * HALF], op=ALU.mult)
+
+        def square(c):
+            nc.scalar.activation(out=gg_t[c][:], in_=g2_t[c][:], func=ACT.Square)
+
+        def slope(c):
+            nc.vector.scalar_tensor_tensor(
+                out=hh_t[c][:], in0=p_t[c][:], scalar=-0.5, in1=gg_t[c][:], op0=ALU.add, op1=ALU.mult
+            )
+
+        def finish(c):
+            h, g = c
+            cols = slice(h * HALF, (h + 1) * HALF)
+            nc.vector.scalar_tensor_tensor(
+                out=y_t[c][:], in0=hh_t[c][:], scalar=gain[:, g, 0:1], in1=base_t[:, g, cols], op0=ALU.mult, op1=ALU.add
+            )
+            nc.sync.dma_start(out=out[g, :, cols], in_=y_t[c][:])
+
+        a, b, c, d = chunks
+        for step, cs in [
+            (root, (a, b)), (share, (a, b)), (centred, (a, b)), (first, (a, b)), (second, (a, b)),
+            (root, (c, d)), (share, (c,)), (square, (a,)), (share, (d,)), (square, (b,)), (centred, (c, d)),
+            (slope, (a, b)), (finish, (a, b)), (first, (c, d)), (second, (c, d)), (square, (c, d)),
+            (slope, (c, d)), (finish, (c, d)),
+        ]:
+            for k in cs:
+                step(k)

@@ -17,6 +17,7 @@ ROWS = D // PACK
 HALF = N // 2
 NT = 128
 SCALAR_COLS = 80
+WARM = 32
 
 FLOPS = 4 * 2 * G * D * M * N
 
@@ -70,29 +71,43 @@ def tile_rows_gptwoshare_kernel(tc, x, w1, w2, w3, re, wo, dy, og, base, out):
                 stop=stop,
             )
 
-        re_t = sb.tile([P, G, 8], F32, name="re_t")
-        og_t = sb.tile([P, G, 8], F32, name="og_t")
-        with nc.allow_non_contiguous_dma(reason="one value a partition"):
-            nc.scalar.dma_start(out=re_t[:, :, 0:1], in_=re.rearrange("g m o -> m g o"))
-            nc.scalar.dma_start(out=og_t[:, :, 0:1], in_=og.rearrange("g m o -> m g o"))
+        rows_t = sb.tile([P, 128], F32, name="rows_t", align_bytes=64)
+        cols_t = sb.tile([P, 128], F32, name="cols_t", align_bytes=64)
+        nc.gpsimd.memset(rows_t[:], 0.0)
+        warm = operand("warm", NT)
+        nc.vector.memset(warm[0][:], 1.0)
+        quantise(warm)
+        warm_bank = ps.tile([P, NT], F32, name="warm_bank")
+        for k in range(WARM):
+            nc.tensor.matmul_mx(
+                out=warm_bank[:], lhsT=warm[1][:].bitcast(FP8X4), lhsT_scale=warm[2][:],
+                rhs=warm[1][:].bitcast(FP8X4), rhs_scale=warm[2][:], start=True, stop=True,
+            )
 
+        x_raw = [load("x_raw0", x, 0, HALF)]
+        for k, vec in enumerate((re, og)):
+            nc.sync.dma_start(
+                out=rows_t[0:P:32, 64 * k : 64 * k + 64].rearrange("q (g i) -> q g i", g=G),
+                in_=vec.rearrange("g (q i) o -> q g (i o)", i=32),
+            )
         w1_raw = load("w1_raw", w1, 0, M)
         w2_raw = load("w2_raw", w2, 0, M)
-        x_raw = [load("x_raw%d" % h, x, h * HALF, HALF) for h in range(2)]
+        x_raw.append(load("x_raw1", x, HALF, HALF))
         w3_raw = load("w3_raw", w3, 0, M)
         wo_raw = load("wo_raw", wo, 0, M)
         dy_raw = [load("dy_raw%d" % h, dy, h * HALF, HALF) for h in range(2)]
         base_t = sb.tile([P, G, N], F32, name="base_t")
         nc.sync.dma_start(out=base_t[:], in_=base.rearrange("g m n -> m g n"))
 
-        w12 = operand("w12", 2 * M)
-        w3o = operand("w3o", 2 * M)
+        w1q, w2q, w3q, woq = [operand(name, M) for name in ("w1q", "w2q", "w3q", "woq")]
         xq = [operand("xq%d" % h, HALF) for h in range(2)]
         dyq = [operand("dyq%d" % h, HALF) for h in range(2)]
 
         chunks = [(h, g) for h in range(2) for g in range(G)]
         e_bank = {c: ps.tile([P, 2 * HALF], F32, name="e_bank%d%d" % c) for c in chunks}
-        a_bank = {c: ps.tile([P, 2 * HALF], F32, name="a_bank%d%d" % c) for c in chunks}
+        a_bank = {(0, g): ps.tile([P, 2 * HALF], F32, name="a_bank%d" % g) for g in range(G)}
+        for g in range(G):
+            a_bank[(1, g)] = e_bank[(0, g)]
 
         def work(name, width=HALF):
             return {c: sb.tile([P, width], F32, name=name + "%d%d" % c) for c in chunks}
@@ -106,56 +121,71 @@ def tile_rows_gptwoshare_kernel(tc, x, w1, w2, w3, re, wo, dy, og, base, out):
             for g in range(G):
                 bank = e_bank[(h, g)]
                 for b in range(HALF // NT):
-                    mm(bank[:, b * NT : (b + 1) * NT], g, w12, 0, xq[h], b * NT, True, True)
+                    mm(bank[:, b * NT : (b + 1) * NT], g, w1q, 0, xq[h], b * NT, True, True)
                 for b in range(HALF // NT):
                     dst = bank[:, HALF + b * NT : HALF + (b + 1) * NT]
-                    mm(dst, g, w12, 0, xq[h], b * NT, True, False)
-                    mm(dst, g, w12, M, xq[h], b * NT, False, True)
+                    mm(dst, g, w1q, 0, xq[h], b * NT, True, False)
+                    mm(dst, g, w2q, 0, xq[h], b * NT, False, True)
 
         def value_matmuls(h, which, aop):
             for g in range(G):
                 for b in range(HALF // NT):
                     dst = a_bank[(h, g)][:, which * HALF + b * NT : which * HALF + (b + 1) * NT]
-                    mm(dst, g, w3o, which * M, aop, b * NT, True, True)
+                    mm(dst, g, (w3q, woq)[which], 0, aop, b * NT, True, True)
 
         def exps(h):
             for g in range(G):
                 nc.scalar.activation(out=e_t[(h, g)][:], in_=e_bank[(h, g)][:], func=ACT.Exp)
 
-        def odds(h):
-            for g in range(G):
-                c = (h, g)
-                nc.vector.scalar_tensor_tensor(
-                    out=t_t[c][:], in0=e_t[c][:, 0:HALF], scalar=re_t[:, g, 0:1], in1=e_t[c][:, HALF : 2 * HALF],
-                    op0=ALU.mult, op1=ALU.add,
-                )
+        def odds(c):
+            g = c[1]
+            nc.vector.scalar_tensor_tensor(
+                out=t_t[c][:], in0=e_t[c][:, 0:HALF], scalar=cols_t[:, 32 * g : 32 * g + 1],
+                in1=e_t[c][:, HALF : 2 * HALF], op0=ALU.mult, op1=ALU.add,
+            )
 
+        a, b, c, d = chunks
+        inter_v(xq[0], x_raw[0], 0, SCALAR_COLS, HALF)
+        inter_s(xq[0], x_raw[0], 0, 0, SCALAR_COLS)
         nc.vector.tensor_scalar(
-            out=w12[0][:, 0:M, :], in0=w1_raw[:].rearrange("p j c -> p c j"), scalar1=-1.0, scalar2=None, op0=ALU.mult
+            out=w1q[0][:, 40:M, :], in0=w1_raw[:, :, 40:M].rearrange("p j c -> p c j"), scalar1=-1.0, scalar2=None,
+            op0=ALU.mult,
         )
-        inter_s(w12, w2_raw, M, 0, M)
-        nc.gpsimd.tensor_scalar(out=gain[:, :, 0:1], in0=og_t[:, :, 0:1], scalar1=-4.0, scalar2=None, op0=ALU.mult)
-        quantise(w12)
-        for h in range(2):
-            inter_v(xq[h], x_raw[h], 0, SCALAR_COLS, HALF)
-            inter_s(xq[h], x_raw[h], 0, 0, SCALAR_COLS)
-            quantise(xq[h])
-            score_matmuls(h)
+        nc.scalar.activation(
+            out=w1q[0][:, 0:40, :], in_=w1_raw[:, :, 0:40].rearrange("p j c -> p c j"), func=ACT.Copy, scale=-1.0
+        )
+        quantise(xq[0])
+        quantise(w1q)
+        inter_v(w2q, w2_raw, 0, 64, M)
+        inter_s(w2q, w2_raw, 0, 0, 64)
+        nc.vector.transpose(out=cols_t[:], in_=rows_t[:])
+        quantise(w2q)
+        nc.gpsimd.tensor_scalar(
+            out=gain[:, :, 0], in0=cols_t[:, 64:128:32], scalar1=-4.0, scalar2=None, op0=ALU.mult
+        )
+        score_matmuls(0)
+        inter_v(xq[1], x_raw[1], 0, SCALAR_COLS, HALF)
+        inter_s(xq[1], x_raw[1], 0, 0, SCALAR_COLS)
+        quantise(xq[1])
+        score_matmuls(1)
         exps(0)
         exps(1)
-        inter_v(w3o, w3_raw, 0, 0, M)
-        inter_v(w3o, wo_raw, M, 0, M)
-        odds(0)
-        quantise(w3o)
+        inter_v(w3q, w3_raw, 0, 0, M)
+        inter_v(woq, wo_raw, 0, 0, M)
+        quantise(w3q)
+        quantise(woq)
         value_matmuls(0, 0, xq[0])
         value_matmuls(1, 0, xq[1])
+        odds(a)
+        odds(b)
         inter_v(dyq[0], dy_raw[0], 0, 0, HALF)
-        odds(1)
+        inter_v(dyq[1], dy_raw[1], 0, 0, HALF)
         quantise(dyq[0])
         value_matmuls(0, 1, dyq[0])
-        inter_v(dyq[1], dy_raw[1], 0, 0, HALF)
         quantise(dyq[1])
         value_matmuls(1, 1, dyq[1])
+        odds(c)
+        odds(d)
 
         def root(c):
             nc.scalar.activation(out=rs_t[c][:], in_=t_t[c][:], func=ACT.Abs_reciprocal_sqrt, bias=1.0)
@@ -190,10 +220,9 @@ def tile_rows_gptwoshare_kernel(tc, x, w1, w2, w3, re, wo, dy, og, base, out):
             )
             nc.sync.dma_start(out=out[g, :, cols], in_=y_t[c][:])
 
-        a, b, c, d = chunks
         for step, cs in [
             (root, (a, b)), (share, (a, b)), (centred, (a, b)), (first, (a, b)), (second, (a, b)),
-            (root, (c, d)), (share, (c,)), (square, (a,)), (share, (d,)), (square, (b,)), (centred, (c, d)),
+            (root, (c, d)), (square, (a, b)), (share, (c, d)), (centred, (c, d)),
             (slope, (a, b)), (finish, (a, b)), (first, (c, d)), (second, (c, d)), (square, (c, d)),
             (slope, (c, d)), (finish, (c, d)),
         ]:

@@ -84,18 +84,19 @@ def tile_rows_gptwoshare_kernel(tc, x, w1, w2, w3, re, wo, dy, og, base, out):
                 rhs=warm[1][:].bitcast(FP8X4), rhs_scale=warm[2][:], start=True, stop=True,
             )
 
+        w1_raw = load("w1_raw", w1, 0, M)
         x_raw = [load("x_raw0", x, 0, HALF)]
         for k, vec in enumerate((re, og)):
             nc.sync.dma_start(
                 out=rows_t[0:P:32, 64 * k : 64 * k + 64].rearrange("q (g i) -> q g i", g=G),
                 in_=vec.rearrange("g (q i) o -> q g (i o)", i=32),
             )
-        w1_raw = load("w1_raw", w1, 0, M)
         w2_raw = load("w2_raw", w2, 0, M)
         x_raw.append(load("x_raw1", x, HALF, HALF))
         w3_raw = load("w3_raw", w3, 0, M)
         wo_raw = load("wo_raw", wo, 0, M)
-        dy_raw = [load("dy_raw%d" % h, dy, h * HALF, HALF) for h in range(2)]
+        dy_all = load("dy_raw", dy, 0, N)
+        dy_raw = [dy_all[:, :, h * HALF : (h + 1) * HALF] for h in range(2)]
         base_t = sb.tile([P, G, N], F32, name="base_t")
         nc.sync.dma_start(out=base_t[:], in_=base.rearrange("g m n -> m g n"))
 
@@ -104,10 +105,11 @@ def tile_rows_gptwoshare_kernel(tc, x, w1, w2, w3, re, wo, dy, og, base, out):
         dyq = [operand("dyq%d" % h, HALF) for h in range(2)]
 
         chunks = [(h, g) for h in range(2) for g in range(G)]
-        e_bank = {c: ps.tile([P, 2 * HALF], F32, name="e_bank%d%d" % c) for c in chunks}
+        z_bank = [ps.tile([P, 2 * HALF], F32, name="z_bank%d" % g) for g in range(G)]
+        d_bank = [ps.tile([P, 2 * HALF], F32, name="d_bank%d" % g) for g in range(G)]
         a_bank = {(0, g): ps.tile([P, 2 * HALF], F32, name="a_bank%d" % g) for g in range(G)}
         for g in range(G):
-            a_bank[(1, g)] = e_bank[(0, g)]
+            a_bank[(1, g)] = z_bank[g]
 
         def work(name, width=HALF):
             return {c: sb.tile([P, width], F32, name=name + "%d%d" % c) for c in chunks}
@@ -117,13 +119,15 @@ def tile_rows_gptwoshare_kernel(tc, x, w1, w2, w3, re, wo, dy, og, base, out):
         g1_t, g2_t, gg_t, hh_t, y_t = work("g1"), work("g2"), work("gg"), work("hh"), work("y")
         gain = sb.tile([P, G, 8], F32, name="gain")
 
-        def score_matmuls(h):
+        def minus_z1(h):
             for g in range(G):
-                bank = e_bank[(h, g)]
                 for b in range(HALF // NT):
-                    mm(bank[:, b * NT : (b + 1) * NT], g, w1q, 0, xq[h], b * NT, True, True)
+                    mm(z_bank[g][:, b * NT : (b + 1) * NT], g, w1q, 0, xq[h], b * NT, True, True)
+
+        def z2_minus_z1(h):
+            for g in range(G):
                 for b in range(HALF // NT):
-                    dst = bank[:, HALF + b * NT : HALF + (b + 1) * NT]
+                    dst = d_bank[g][:, b * NT : (b + 1) * NT]
                     mm(dst, g, w1q, 0, xq[h], b * NT, True, False)
                     mm(dst, g, w2q, 0, xq[h], b * NT, False, True)
 
@@ -133,9 +137,11 @@ def tile_rows_gptwoshare_kernel(tc, x, w1, w2, w3, re, wo, dy, og, base, out):
                     dst = a_bank[(h, g)][:, which * HALF + b * NT : which * HALF + (b + 1) * NT]
                     mm(dst, g, (w3q, woq)[which], 0, aop, b * NT, True, True)
 
-        def exps(h):
+        def exps(h, which, banks):
             for g in range(G):
-                nc.scalar.activation(out=e_t[(h, g)][:], in_=e_bank[(h, g)][:], func=ACT.Exp)
+                nc.scalar.activation(
+                    out=e_t[(h, g)][:, which * HALF : (which + 1) * HALF], in_=banks[g][:, 0:HALF], func=ACT.Exp
+                )
 
         def odds(c):
             g = c[1]
@@ -145,8 +151,6 @@ def tile_rows_gptwoshare_kernel(tc, x, w1, w2, w3, re, wo, dy, og, base, out):
             )
 
         a, b, c, d = chunks
-        inter_v(xq[0], x_raw[0], 0, SCALAR_COLS, HALF)
-        inter_s(xq[0], x_raw[0], 0, 0, SCALAR_COLS)
         nc.vector.tensor_scalar(
             out=w1q[0][:, 40:M, :], in0=w1_raw[:, :, 40:M].rearrange("p j c -> p c j"), scalar1=-1.0, scalar2=None,
             op0=ALU.mult,
@@ -154,38 +158,47 @@ def tile_rows_gptwoshare_kernel(tc, x, w1, w2, w3, re, wo, dy, og, base, out):
         nc.scalar.activation(
             out=w1q[0][:, 0:40, :], in_=w1_raw[:, :, 0:40].rearrange("p j c -> p c j"), func=ACT.Copy, scale=-1.0
         )
-        quantise(xq[0])
         quantise(w1q)
-        inter_v(w2q, w2_raw, 0, 64, M)
-        inter_s(w2q, w2_raw, 0, 0, 64)
+        inter_v(xq[0], x_raw[0], 0, SCALAR_COLS, HALF)
+        inter_s(xq[0], x_raw[0], 0, 0, SCALAR_COLS)
         nc.vector.transpose(out=cols_t[:], in_=rows_t[:])
-        quantise(w2q)
+        quantise(xq[0])
         nc.gpsimd.tensor_scalar(
             out=gain[:, :, 0], in0=cols_t[:, 64:128:32], scalar1=-4.0, scalar2=None, op0=ALU.mult
         )
-        score_matmuls(0)
-        inter_v(xq[1], x_raw[1], 0, SCALAR_COLS, HALF)
-        inter_s(xq[1], x_raw[1], 0, 0, SCALAR_COLS)
+        inter_s(w2q, w2_raw, 0, 0, M)
+        quantise(w2q)
+        minus_z1(0)
+        z2_minus_z1(0)
+        exps(0, 0, z_bank)
+        exps(0, 1, d_bank)
+        inter_v(xq[1], x_raw[1], 0, 0, HALF)
         quantise(xq[1])
-        score_matmuls(1)
-        exps(0)
-        exps(1)
+        minus_z1(1)
+        z2_minus_z1(1)
+        exps(1, 0, z_bank)
+        exps(1, 1, d_bank)
         inter_v(w3q, w3_raw, 0, 0, M)
         inter_v(woq, wo_raw, 0, 0, M)
         quantise(w3q)
         quantise(woq)
         value_matmuls(0, 0, xq[0])
         value_matmuls(1, 0, xq[1])
-        odds(a)
-        odds(b)
+        for k in chunks:
+            odds(k)
         inter_v(dyq[0], dy_raw[0], 0, 0, HALF)
-        inter_v(dyq[1], dy_raw[1], 0, 0, HALF)
         quantise(dyq[0])
         value_matmuls(0, 1, dyq[0])
-        quantise(dyq[1])
-        value_matmuls(1, 1, dyq[1])
-        odds(c)
-        odds(d)
+
+        def share_v(c):
+            nc.vector.tensor_tensor(out=p_t[c][:], in0=rs_t[c][:], in1=rs_t[c][:], op=ALU.mult)
+
+        def dy_inter(h):
+            inter_v(dyq[h], dy_raw[h], 0, 0, HALF)
+
+        def dy_quant(h):
+            quantise(dyq[h])
+            value_matmuls(h, 1, dyq[h])
 
         def root(c):
             nc.scalar.activation(out=rs_t[c][:], in_=t_t[c][:], func=ACT.Abs_reciprocal_sqrt, bias=1.0)
@@ -220,11 +233,37 @@ def tile_rows_gptwoshare_kernel(tc, x, w1, w2, w3, re, wo, dy, og, base, out):
             )
             nc.sync.dma_start(out=out[g, :, cols], in_=y_t[c][:])
 
-        for step, cs in [
-            (root, (a, b)), (share, (a, b)), (centred, (a, b)), (first, (a, b)), (second, (a, b)),
-            (root, (c, d)), (square, (a, b)), (share, (c, d)), (centred, (c, d)),
-            (slope, (a, b)), (finish, (a, b)), (first, (c, d)), (second, (c, d)), (square, (c, d)),
-            (slope, (c, d)), (finish, (c, d)),
-        ]:
-            for k in cs:
-                step(k)
+        root(a)
+        root(b)
+        share_v(a)
+        share_v(b)
+        dy_inter(1)
+        centred(a)
+        centred(b)
+        root(c)
+        root(d)
+        share(c)
+        share(d)
+        first(a)
+        first(b)
+        second(a)
+        second(b)
+        dy_quant(1)
+        centred(c)
+        centred(d)
+        square(a)
+        square(b)
+        first(c)
+        first(d)
+        slope(a)
+        slope(b)
+        second(c)
+        second(d)
+        square(c)
+        square(d)
+        finish(a)
+        finish(b)
+        slope(c)
+        slope(d)
+        finish(c)
+        finish(d)

@@ -100,7 +100,8 @@ def tile_rows_gptwoshare_kernel(tc, x, w1, w2, w3, re, wo, dy, og, base, out):
         base_t = sb.tile([P, G, N], F32, name="base_t")
         nc.sync.dma_start(out=base_t[:], in_=base.rearrange("g m n -> m g n"))
 
-        w1q, w2q, w3q, woq = [operand(name, M) for name in ("w1q", "w2q", "w3q", "woq")]
+        w1q, w2q = [operand(name, M) for name in ("w1q", "w2q")]
+        w3o = operand("w3o", 2 * M)
         xq = [operand("xq%d" % h, HALF) for h in range(2)]
         dyq = [operand("dyq%d" % h, HALF) for h in range(2)]
 
@@ -135,10 +136,10 @@ def tile_rows_gptwoshare_kernel(tc, x, w1, w2, w3, re, wo, dy, og, base, out):
             for g in range(G):
                 for b in range(HALF // NT):
                     dst = a_bank[(h, g)][:, which * HALF + b * NT : which * HALF + (b + 1) * NT]
-                    mm(dst, g, (w3q, woq)[which], 0, aop, b * NT, True, True)
+                    mm(dst, g, w3o, which * M, aop, b * NT, True, True)
 
-        def exps(h, which, banks):
-            for g in range(G):
+        def exps(h, which, banks, groups=(0, 1)):
+            for g in groups:
                 nc.scalar.activation(
                     out=e_t[(h, g)][:, which * HALF : (which + 1) * HALF], in_=banks[g][:, 0:HALF], func=ACT.Exp
                 )
@@ -163,32 +164,36 @@ def tile_rows_gptwoshare_kernel(tc, x, w1, w2, w3, re, wo, dy, og, base, out):
         inter_s(xq[0], x_raw[0], 0, 0, SCALAR_COLS)
         nc.vector.transpose(out=cols_t[:], in_=rows_t[:])
         quantise(xq[0])
-        nc.gpsimd.tensor_scalar(
-            out=gain[:, :, 0], in0=cols_t[:, 64:128:32], scalar1=-4.0, scalar2=None, op0=ALU.mult
-        )
+        nc.scalar.activation(out=gain[:, :, 0], in_=cols_t[:, 64:128:32], func=ACT.Copy, scale=-4.0)
         inter_s(w2q, w2_raw, 0, 0, M)
         quantise(w2q)
         minus_z1(0)
         z2_minus_z1(0)
-        exps(0, 0, z_bank)
+        exps(0, 0, z_bank, (0,))
+        inter_v(xq[1], x_raw[1], 0, 48, HALF)
+        inter_s(xq[1], x_raw[1], 0, 0, 48)
+        exps(0, 0, z_bank, (1,))
         exps(0, 1, d_bank)
-        inter_v(xq[1], x_raw[1], 0, 0, HALF)
         quantise(xq[1])
         minus_z1(1)
         z2_minus_z1(1)
         exps(1, 0, z_bank)
         exps(1, 1, d_bank)
-        inter_v(w3q, w3_raw, 0, 0, M)
-        inter_v(woq, wo_raw, 0, 0, M)
-        quantise(w3q)
-        quantise(woq)
+        inter_v(w3o, w3_raw, 0, 0, M)
+        inter_v(w3o, wo_raw, M, 0, M)
+        odds(a)
+        quantise(w3o)
         value_matmuls(0, 0, xq[0])
         value_matmuls(1, 0, xq[1])
-        for k in chunks:
-            odds(k)
-        inter_v(dyq[0], dy_raw[0], 0, 0, HALF)
-        quantise(dyq[0])
-        value_matmuls(0, 1, dyq[0])
+        odds(b)
+        nc.vector.scalar_tensor_tensor(
+            out=rs_t[a][:], in0=t_t[a][:], scalar=2.0, in1=t_t[a][:], op0=ALU.add, op1=ALU.mult
+        )
+        odds(c)
+        odds(d)
+
+        def direct(c):
+            nc.scalar.activation(out=p_t[c][:], in_=rs_t[c][:], func=ACT.Abs_reciprocal_sqrt, bias=1.0)
 
         def share_v(c):
             nc.vector.tensor_tensor(out=p_t[c][:], in0=rs_t[c][:], in1=rs_t[c][:], op=ALU.mult)
@@ -233,35 +238,36 @@ def tile_rows_gptwoshare_kernel(tc, x, w1, w2, w3, re, wo, dy, og, base, out):
             )
             nc.sync.dma_start(out=out[g, :, cols], in_=y_t[c][:])
 
-        root(a)
-        root(b)
-        share_v(a)
-        share_v(b)
+        dy_inter(0)
         dy_inter(1)
-        centred(a)
-        centred(b)
-        root(c)
-        root(d)
-        share(c)
-        share(d)
-        first(a)
-        first(b)
-        second(a)
-        second(b)
+        dy_quant(0)
         dy_quant(1)
+        direct(a)
+        root(b)
+        centred(a)
+        share(b)
+        root(c)
+        centred(b)
+        share(c)
+        root(d)
+        first(a)
+        second(a)
         centred(c)
-        centred(d)
         square(a)
+        first(b)
+        share(d)
+        second(b)
         square(b)
+        centred(d)
         first(c)
-        first(d)
         slope(a)
-        slope(b)
         second(c)
-        second(d)
         square(c)
-        square(d)
         finish(a)
+        first(d)
+        slope(b)
+        second(d)
+        square(d)
         finish(b)
         slope(c)
         slope(d)

@@ -17,7 +17,6 @@ ROWS = D // PACK
 HALF = N // 2
 NT = 128
 SCALAR_COLS = 80
-WARM = 32
 
 FLOPS = 4 * 2 * G * D * M * N
 
@@ -74,15 +73,6 @@ def tile_rows_gptwoshare_kernel(tc, x, w1, w2, w3, re, wo, dy, og, base, out):
         rows_t = sb.tile([P, 128], F32, name="rows_t", align_bytes=64)
         cols_t = sb.tile([P, 128], F32, name="cols_t", align_bytes=64)
         nc.gpsimd.memset(rows_t[:], 0.0)
-        warm = operand("warm", NT)
-        nc.vector.memset(warm[0][:], 1.0)
-        quantise(warm)
-        warm_bank = ps.tile([P, NT], F32, name="warm_bank")
-        for k in range(WARM):
-            nc.tensor.matmul_mx(
-                out=warm_bank[:], lhsT=warm[1][:].bitcast(FP8X4), lhsT_scale=warm[2][:],
-                rhs=warm[1][:].bitcast(FP8X4), rhs_scale=warm[2][:], start=True, stop=True,
-            )
 
         w1_raw = load("w1_raw", w1, 0, M)
         x_raw = [load("x_raw0", x, 0, HALF)]

from contextlib import ExitStack

import concourse.mybir as mybir

F32 = mybir.dt.float32
BF16 = mybir.dt.bfloat16
U32 = mybir.dt.uint32
U8 = mybir.dt.uint8
FP8X4 = mybir.dt.float8_e4m3fn_x4
ACT = mybir.ActivationFunctionType
ALU = mybir.AluOpType

G, D, M, N = 2, 256, 128, 512
P = 128
PACK = 4
ROWS = D // PACK
HALF = N // 2
NT = 128
SCALAR_COLS = 80

FLOPS = 4 * 2 * G * D * M * N


def tile_rows_gptwoshare_kernel(tc, x, w1, w2, w3, re, wo, dy, og, base, out):
    nc = tc.nc
    with ExitStack() as ctx:
        sb = ctx.enter_context(tc.tile_pool(name="sb", bufs=1))
        ps = ctx.enter_context(tc.psum_pool(name="ps", bufs=1))
        ctx.enter_context(tc.manual_schedule())

        def load(name, src, c0, width):
            raw = sb.tile([P, PACK, width], F32, name=name, align_bytes=64)
            view = src.rearrange("g (p j) c -> (g p) j c", j=PACK)
            nc.sync.dma_start(out=raw[:], in_=view[:, :, c0 : c0 + width])
            return raw

        def operand(name, width):
            grouped = sb.tile([P, width, PACK], BF16, name=name + "_b", align_bytes=64)
            codes = sb.tile([P, width], U32, name=name + "_c", align_bytes=64)
            scales = sb.tile([P, width], U8, name=name + "_s", align_bytes=64)
            return grouped, codes, scales

        def views(op, raw, dst0, c0, c1):
            dst = op[0][:, dst0 + c0 : dst0 + c1, :].rearrange("p (c i) j -> p c j i", i=4)
            src = raw[:, :, c0:c1].rearrange("p j (c i) -> p c j i", i=4)
            return dst, src

        def inter_v(op, raw, dst0, c0, c1):
            dst, src = views(op, raw, dst0, c0, c1)
            nc.vector.tensor_copy(out=dst, in_=src)

        def inter_s(op, raw, dst0, c0, c1):
            dst, src = views(op, raw, dst0, c0, c1)
            nc.scalar.copy(out=dst, in_=src)

        def quantise(op):
            nc.vector.quantize_mx(
                out=op[1][:].bitcast(FP8X4), scales=op[2][:], in_=op[0][:].rearrange("p c j -> p (c j)")
            )

        def mm(dst, g, wop, w0, aop, a0, start, stop):
            rows = slice(g * ROWS, (g + 1) * ROWS)
            nc.tensor.matmul_mx(
                out=dst,
                lhsT=wop[1][rows, w0 : w0 + M].bitcast(FP8X4),
                lhsT_scale=wop[2][rows, w0 : w0 + M],
                rhs=aop[1][rows, a0 : a0 + NT].bitcast(FP8X4),
                rhs_scale=aop[2][rows, a0 : a0 + NT],
                start=start,
                stop=stop,
            )

        rows_t = sb.tile([P, 128], F32, name="rows_t", align_bytes=64)
        cols_t = sb.tile([P, 128], F32, name="cols_t", align_bytes=64)
        nc.gpsimd.memset(rows_t[:], 0.0)

        w1_raw = load("w1_raw", w1, 0, M)
        x_raw = [load("x_raw0", x, 0, HALF)]
        for k, vec in enumerate((re, og)):
            nc.sync.dma_start(
                out=rows_t[0:P:32, 64 * k : 64 * k + 64].rearrange("q (g i) -> q g i", g=G),
                in_=vec.rearrange("g (q i) o -> q g (i o)", i=32),
            )
        w2_raw = load("w2_raw", w2, 0, M)
        x_raw.append(load("x_raw1", x, HALF, HALF))
        w3_raw = load("w3_raw", w3, 0, M)
        wo_raw = load("wo_raw", wo, 0, M)
        dy_all = load("dy_raw", dy, 0, N)
        dy_raw = [dy_all[:, :, h * HALF : (h + 1) * HALF] for h in range(2)]
        base_t = sb.tile([P, G, N], F32, name="base_t")
        nc.sync.dma_start(out=base_t[:], in_=base.rearrange("g m n -> m g n"))

        w1q, w2q = [operand(name, M) for name in ("w1q", "w2q")]
        w3o = operand("w3o", 2 * M)
        xq = [operand("xq%d" % h, HALF) for h in range(2)]
        dyq = [operand("dyq%d" % h, HALF) for h in range(2)]

        chunks = [(h, g) for h in range(2) for g in range(G)]
        z_bank = [ps.tile([P, 2 * HALF], F32, name="z_bank%d" % g) for g in range(G)]
        d_bank = [ps.tile([P, 2 * HALF], F32, name="d_bank%d" % g) for g in range(G)]
        a_bank = {(0, g): ps.tile([P, 2 * HALF], F32, name="a_bank%d" % g) for g in range(G)}
        for g in range(G):
            a_bank[(1, g)] = z_bank[g]

        def work(name, width=HALF):
            return {c: sb.tile([P, width], F32, name=name + "%d%d" % c) for c in chunks}

        e_t = work("e", 2 * HALF)
        t_t, rs_t, p_t, h2_t = work("t"), work("rs"), work("p"), work("h2")
        g1_t, g2_t, gg_t, hh_t, y_t = work("g1"), work("g2"), work("gg"), work("hh"), work("y")
        gain = sb.tile([P, G, 8], F32, name="gain")

        def minus_z1(h):
            for g in range(G):
                for b in range(HALF // NT):
                    mm(z_bank[g][:, b * NT : (b + 1) * NT], g, w1q, 0, xq[h], b * NT, True, True)

        def z2_minus_z1(h):
            for g in range(G):
                for b in range(HALF // NT):
                    dst = d_bank[g][:, b * NT : (b + 1) * NT]
                    mm(dst, g, w1q, 0, xq[h], b * NT, True, False)
                    mm(dst, g, w2q, 0, xq[h], b * NT, False, True)

        def value_matmuls(h, which, aop):
            for g in range(G):
                for b in range(HALF // NT):
                    dst = a_bank[(h, g)][:, which * HALF + b * NT : which * HALF + (b + 1) * NT]
                    mm(dst, g, w3o, which * M, aop, b * NT, True, True)

        def exps(h, which, banks, groups=(0, 1)):
            for g in groups:
                nc.scalar.activation(
                    out=e_t[(h, g)][:, which * HALF : (which + 1) * HALF], in_=banks[g][:, 0:HALF], func=ACT.Exp
                )

        def odds(c):
            g = c[1]
            nc.vector.scalar_tensor_tensor(
                out=t_t[c][:], in0=e_t[c][:, 0:HALF], scalar=cols_t[:, 32 * g : 32 * g + 1],
                in1=e_t[c][:, HALF : 2 * HALF], op0=ALU.mult, op1=ALU.add,
            )

        a, b, c, d = chunks
        nc.vector.tensor_scalar(
            out=w1q[0][:, 40:M, :], in0=w1_raw[:, :, 40:M].rearrange("p j c -> p c j"), scalar1=-1.0, scalar2=None,
            op0=ALU.mult,
        )
        nc.scalar.activation(
            out=w1q[0][:, 0:40, :], in_=w1_raw[:, :, 0:40].rearrange("p j c -> p c j"), func=ACT.Copy, scale=-1.0
        )
        quantise(w1q)
        inter_v(xq[0], x_raw[0], 0, SCALAR_COLS, HALF)
        inter_s(xq[0], x_raw[0], 0, 0, SCALAR_COLS)
        nc.vector.transpose(out=cols_t[:], in_=rows_t[:])
        quantise(xq[0])
        nc.scalar.activation(out=gain[:, :, 0], in_=cols_t[:, 64:128:32], func=ACT.Copy, scale=-4.0)
        inter_s(w2q, w2_raw, 0, 0, M)
        quantise(w2q)
        minus_z1(0)
        z2_minus_z1(0)
        exps(0, 0, z_bank, (0,))
        inter_v(xq[1], x_raw[1], 0, 48, HALF)
        inter_s(xq[1], x_raw[1], 0, 0, 48)
        exps(0, 0, z_bank, (1,))
        exps(0, 1, d_bank)
        quantise(xq[1])
        minus_z1(1)
        z2_minus_z1(1)
        exps(1, 0, z_bank)
        exps(1, 1, d_bank)
        inter_v(w3o, w3_raw, 0, 0, M)
        inter_v(w3o, wo_raw, M, 0, M)
        odds(a)
        quantise(w3o)
        value_matmuls(0, 0, xq[0])
        value_matmuls(1, 0, xq[1])
        odds(b)
        nc.vector.scalar_tensor_tensor(
            out=rs_t[a][:], in0=t_t[a][:], scalar=2.0, in1=t_t[a][:], op0=ALU.add, op1=ALU.mult
        )
        odds(c)
        odds(d)

        def direct(c):
            nc.scalar.activation(out=p_t[c][:], in_=rs_t[c][:], func=ACT.Abs_reciprocal_sqrt, bias=1.0)

        def share_v(c):
            nc.vector.tensor_tensor(out=p_t[c][:], in0=rs_t[c][:], in1=rs_t[c][:], op=ALU.mult)

        def dy_inter(h):
            inter_v(dyq[h], dy_raw[h], 0, 0, HALF)

        def dy_quant(h):
            quantise(dyq[h])
            value_matmuls(h, 1, dyq[h])

        def root(c):
            nc.scalar.activation(out=rs_t[c][:], in_=t_t[c][:], func=ACT.Abs_reciprocal_sqrt, bias=1.0)

        def share(c):
            nc.scalar.activation(out=p_t[c][:], in_=rs_t[c][:], func=ACT.Square)

        def centred(c):
            nc.scalar.activation(out=h2_t[c][:], in_=p_t[c][:], func=ACT.Square, bias=-0.5)

        def first(c):
            nc.vector.scalar_tensor_tensor(
                out=g1_t[c][:], in0=h2_t[c][:], scalar=-0.25, in1=a_bank[c][:, 0:HALF], op0=ALU.add, op1=ALU.mult
            )

        def second(c):
            nc.vector.tensor_tensor(out=g2_t[c][:], in0=g1_t[c][:], in1=a_bank[c][:, HALF : 2 * HALF], op=ALU.mult)

        def square(c):
            nc.scalar.activation(out=gg_t[c][:], in_=g2_t[c][:], func=ACT.Square)

        def slope(c):
            nc.vector.scalar_tensor_tensor(
                out=hh_t[c][:], in0=p_t[c][:], scalar=-0.5, in1=gg_t[c][:], op0=ALU.add, op1=ALU.mult
            )

        def finish(c):
            h, g = c
            cols = slice(h * HALF, (h + 1) * HALF)
            nc.vector.scalar_tensor_tensor(
                out=y_t[c][:], in0=hh_t[c][:], scalar=gain[:, g, 0:1], in1=base_t[:, g, cols], op0=ALU.mult, op1=ALU.add
            )
            nc.sync.dma_start(out=out[g, :, cols], in_=y_t[c][:])

        dy_inter(0)
        dy_inter(1)
        dy_quant(0)
        dy_quant(1)
        direct(a)
        root(b)
        centred(a)
        share(b)
        root(c)
        centred(b)
        share(c)
        root(d)
        first(a)
        second(a)
        centred(c)
        square(a)
        first(b)
        share(d)
        second(b)
        square(b)
        centred(d)
        first(c)
        slope(a)
        second(c)
        square(c)
        finish(a)
        first(d)
        slope(b)
        second(d)
        square(d)
        finish(b)
        slope(c)
        slope(d)
        finish(c)
        finish(d)
